import numpy as np
import ml_dtypes


def mxq(x, axis, fmt="e4m3"):
    dtype, down = {"e4m3": (ml_dtypes.float8_e4m3fn, 7), "e5m2": (ml_dtypes.float8_e5m2, 14)}[fmt]
    v = np.moveaxis(np.asarray(x, np.float32).astype(ml_dtypes.bfloat16).astype(np.float64), axis, -1)
    blocks = v.reshape(v.shape[:-1] + (-1, 32))
    amax = np.abs(blocks).max(-1, keepdims=True)
    byte = np.maximum(np.where(amax > 0, np.frexp(amax)[1] - 1 + 127, 0) - down, 1)
    scale = np.exp2(byte - 127.0)
    codes = (blocks / scale).astype(np.float32).astype(dtype).astype(np.float64)
    return np.moveaxis((codes * scale).reshape(v.shape), -1, axis)


WIDE = False


def mx_kscale(k):
    if not WIDE:
        return np.ones(k)
    levels = np.array([10, -10, 5, -5, 0])
    if k % 512:
        return np.exp2(np.random.permutation(np.resize(levels, k // 32))).repeat(32)
    a = np.empty((k // 512, 16))
    for p in range(k // 512):
        a[p, :8] = np.random.permutation(np.resize(levels, 8))
        for g in range(8):
            far = levels[np.abs(levels - a[p, g]) >= 10]
            a[p, g + 8] = far[np.random.randint(len(far))]
    return np.exp2(a.ravel()).repeat(32)


def f64(x):
    return np.asarray(x).astype(np.float64)


def striped(idx):
    return np.tile(idx.reshape(-1, 16).T, (8, 1)).astype(np.uint16)


def unstriped(offs):
    return offs[:16].T.reshape(-1).astype(np.int64)


def striped8(idx):
    return np.concatenate([x.reshape(-1, 16).T for x in idx]).astype(np.uint16)


def runs(offs, k):
    lists = np.stack([offs[16 * r : 16 * r + 16].T.reshape(-1) for r in range(8)]).astype(np.int64)
    return lists[np.arange(k) % 512 // 64]


def pack_weight(w):
    k, n = w.shape
    w = f64(np.asarray(w, np.float32).astype(ml_dtypes.bfloat16)).reshape(k // 32, 32, n)
    amax = np.abs(w).max(1)
    byte = np.clip(np.where(amax > 0, np.frexp(amax)[1] - 1 + 127 - 7, 1), 1, 254)
    scaled = (w * np.exp2(127.0 - byte)[:, None, :]).reshape(k, n).astype(np.float32)
    words = np.ascontiguousarray(scaled.reshape(k // 512, 128, 4, n).transpose(0, 1, 3, 2)).astype(ml_dtypes.float8_e4m3fn).view(np.uint8)
    return words, np.ascontiguousarray(byte.astype(np.uint8).reshape(k // 512, 16, n))


def unpack_weight(words, scales):
    g, p, n, _ = words.shape
    vals = np.ascontiguousarray(words).view(ml_dtypes.float8_e4m3fn).astype(np.float64) * np.repeat(np.exp2(scales.astype(np.float64) - 127.0), 8, axis=1)[..., None]
    return vals.transpose(0, 1, 3, 2).reshape(g * 512, n)


E2M1 = np.array([0.0, 0.5, 1.0, 1.5, 2.0, 3.0, 4.0, 6.0, -0.0, -0.5, -1.0, -1.5, -2.0, -3.0, -4.0, -6.0])


def pack_fp4(w):
    k, n = w.shape
    w = f64(np.asarray(w, np.float32).astype(ml_dtypes.bfloat16)).reshape(k // 32, 32, n)
    amax = np.abs(w).max(1)
    mant, ex = np.frexp(amax / 6.0)
    byte = np.clip(np.where(amax > 0, np.where(mant > 0.5, ex, ex - 1) + 127, 1), 1, 254)
    scaled = (w * np.exp2(127.0 - byte)[:, None, :]).reshape(k, n).astype(np.float32)
    c = np.ascontiguousarray(scaled.reshape(k // 512, 128, 4, n).transpose(0, 1, 3, 2)).astype(ml_dtypes.float4_e2m1fn).view(np.uint8) & 0xF
    words = (c[..., 0::2] | (c[..., 1::2] << 4)).reshape(k // 512, 128, 2 * n)
    return np.ascontiguousarray(words), np.ascontiguousarray(byte.astype(np.uint8).reshape(k // 512, 16, n))


def unpack_fp4(words, scales):
    g, _, n = scales.shape
    words = np.ascontiguousarray(words).reshape(g, 128, n, 2)
    nib = np.empty((g, 128, n, 4), np.uint8)
    nib[..., 0::2] = words & 0xF
    nib[..., 1::2] = words >> 4
    vals = E2M1[nib] * np.repeat(np.exp2(scales.astype(np.float64) - 127.0), 8, axis=1)[..., None]
    return vals.transpose(0, 1, 3, 2).reshape(g * 512, n)


def planes(y):
    n, m = y.shape
    v = y.astype(np.float32).astype(ml_dtypes.bfloat16).astype(np.float64).reshape(n // 32, 32, m)
    top = np.abs(v).max(1)
    byte = np.clip(np.where(top > 0, np.frexp(top)[1] - 1 + 127 - 7, 1), 1, 254)
    codes = (v * np.exp2(127.0 - byte)[:, None, :]).reshape(n, m).astype(np.float32).astype(ml_dtypes.float8_e4m3fn).view(np.uint8)
    words = codes.reshape(n // 512, 128, 4, m).transpose(0, 1, 3, 2)
    return np.ascontiguousarray(words), np.ascontiguousarray(byte.astype(np.uint8).reshape(n // 512, 16, m))


K, T, S, H, C, W = 512, 2048, 512, 512, 512, 256


def setup_inputs():
    n = np.random.standard_normal
    s = mx_kscale(K)[:, None]
    packed_xT = pack_weight(n((K, T)) * s)
    packed_w1 = pack_fp4(n((K, H)) / np.sqrt(K) / s)
    perm = np.stack([np.random.permutation(S) for _ in range(8)])
    return {
        "x_words": packed_xT[0],
        "x_scales": packed_xT[1],
        "w1_words": packed_w1[0],
        "w1_scales": packed_w1[1],
        "gs": (np.random.uniform(0.5, 1.5, (K, 1)) / s).astype(np.float32),
        "offs": striped(np.random.permutation(T)[:S]),
        "n1": striped8(np.stack([np.random.permutation(S) for _ in range(8)])),
        "n2": striped8(np.stack([np.random.permutation(S) for _ in range(8)])),
        "cand": striped(np.random.permutation(T)[:C]),
        "n3": striped8(perm[:, :W]),
        "n4": striped8(perm[:, W:]),
        "n5": striped8(np.stack([np.random.permutation(S) for _ in range(8)])),
    }


def reference(x_words, x_scales, w1_words, w1_scales, gs, offs, n1, n2, cand, n3, n4, n5):
    x_cand = unpack_weight(x_words, x_scales)[:, unstriped(cand)]
    xq = unpack_weight(x_words, x_scales)[:, unstriped(offs)]
    y = unpack_fp4(w1_words, w1_scales).T @ xq
    z = f64(gs) * (y[np.arange(H)[:, None], runs(n1, H)] + 0.75 * (y[np.arange(H)[:, None], runs(n2, H)]))
    s = 0.0625 * ((x_cand.T @ mxq(z, 0, "e4m3")))
    pa = s[np.arange(C)[:, None], runs(n3, C)]
    pb = s[np.arange(C)[:, None], runs(n4, C)]
    ra = pa - (0.5 * pb)
    ds = s.copy()
    ds[np.arange(C)[:, None], runs(n4, C)] = ra
    out_0 = ds - (0.5 * (ds[np.arange(C)[:, None], runs(n5, C)]))
    return (out_0,) + planes(out_0)

@@ -1,0 +1,208 @@
+from contextlib import ExitStack
+
+import concourse.mybir as mybir
+
+K, T, S, H, C, W = 512, 2048, 512, 512, 512, 256
+FLOPS = 2 * K * H * S + 2 * K * C * S
+
+F32 = mybir.dt.float32
+BF16 = mybir.dt.bfloat16
+I32 = mybir.dt.int32
+U32 = mybir.dt.uint32
+U16 = mybir.dt.uint16
+U8 = mybir.dt.uint8
+FP8X4 = mybir.dt.float8_e4m3fn_x4
+FP4X4 = mybir.dt.float4_e2m1fn_x4
+MULT = mybir.AluOpType.mult
+ADD = mybir.AluOpType.add
+COPY = mybir.ActivationFunctionType.Copy
+
+P = 128
+PACK = 4
+HALF = S // 2
+VCOLS = 160
+
+
+def tile_picked_candsumfoldd_none_po_kernel(
+    tc, x_words, x_scales, w1_words, w1_scales, gs, offs, n1, n2, cand, n3, n4, n5, out_0, out_1, out_2
+):
+    nc = tc.nc
+    with ExitStack() as ctx:
+        keep = ctx.enter_context(tc.tile_pool(name="keep", bufs=1))
+        psum = ctx.enter_context(tc.psum_pool(name="psum", bufs=1))
+
+        def tile(shape, dtype, name, tag=None):
+            return keep.tile(shape, dtype, name=name, tag=tag or name, align_bytes=64)
+
+        def load_list(src, name):
+            lst = tile([P, src.shape[1]], U16, name)
+            nc.sync.dma_start(lst[:], src)
+            return lst
+
+        def load_scales(src, name, queue):
+            width = src.shape[2]
+            plane = tile([P, width], U8, name)
+            for q in range(4):
+                queue.dma_start(
+                    out=plane[32 * q : 32 * q + 32, :].bitcast(I32),
+                    in_=src[0, 4 * q : 4 * q + 4, :].bitcast(I32).partition_broadcast(8),
+                )
+            return plane
+
+        offs_sb = load_list(offs, "offs_sb")
+        xs = load_scales(x_scales, "xs", nc.sync)
+        cand_sb = load_list(cand, "cand_sb")
+        xw = tile([P, T], U32, "xw")
+        nc.sync.dma_start(out=xw[:].bitcast(I32), in_=x_words[0].rearrange("p c r -> p (c r)").bitcast(I32))
+        ww = tile([P, 2 * H], U8, "ww")
+        nc.sync.dma_start(out=ww[:].bitcast(I32), in_=w1_words[0].bitcast(I32))
+        ws = load_scales(w1_scales, "ws", nc.sync)
+        gs_sb = tile([P, PACK], F32, "gs_sb")
+        nc.sync.dma_start(out=gs_sb[:], in_=gs.rearrange("(p t) o -> p (t o)", t=PACK))
+        n1_sb = load_list(n1, "n1_sb")
+        n2_sb = load_list(n2, "n2_sb")
+        n3_sb = load_list(n3, "n3_sb")
+        n4_sb = load_list(n4, "n4_sb")
+        n5_sb = load_list(n5, "n5_sb")
+
+        q_scales = tile([P, S], U8, "q_scales")
+        nc.vector.tensor_copy(q_scales[:], xs[:].indirect(offs_sb[:]))
+        wwd = tile([P, 2 * H], U8, "wwd")
+        nc.vector.tensor_copy(
+            wwd[:].rearrange("p (t m b) -> p t m b", t=PACK, b=2), ww[:].rearrange("p (m t b) -> p t m b", t=PACK, b=2)
+        )
+        q_words = tile([P, S], U32, "q_words")
+        nc.vector.tensor_copy(q_words[:], xw[:].indirect(offs_sb[:]))
+        wsd = tile([P, H], U8, "wsd")
+        nc.vector.tensor_copy(wsd[:].rearrange("p (t m) -> p t m", t=PACK), ws[:].rearrange("p (m t) -> p t m", t=PACK))
+        c_scales = tile([P, C], U8, "c_scales")
+        nc.vector.tensor_copy(c_scales[:], xs[:].indirect(cand_sb[:]))
+        c_words = tile([P, C], U32, "c_words", tag="ws")
+        nc.vector.tensor_copy(c_words[:], xw[:].indirect(cand_sb[:]))
+        csd = tile([P, C], U8, "csd")
+        nc.vector.tensor_copy(csd[:].rearrange("p (t m) -> p t m", t=PACK), c_scales[:].rearrange("p (m t) -> p t m", t=PACK))
+        cwd = tile([P, C], U32, "cwd")
+        nc.vector.tensor_copy(cwd[:].rearrange("p (t m) -> p m t", t=PACK), c_words[:].rearrange("p (m t) -> p m t", t=PACK))
+
+        gy = []
+        for t in range(PACK):
+            acc = psum.tile([P, S], F32, name=f"acc_y{t}", tag=f"bank{t}")
+            nc.tensor.matmul_mx(
+                out=acc[:],
+                lhsT=wwd[:, 2 * P * t : 2 * P * (t + 1)].bitcast(FP4X4),
+                lhsT_scale=wsd[:, P * t : P * (t + 1)],
+                rhs=q_words[:].bitcast(FP8X4),
+                rhs_scale=q_scales[:],
+                start=True,
+                stop=True,
+            )
+            gy_t = tile([P, S], F32, f"gy{t}")
+            nc.scalar.activation(gy_t[:], acc[:], COPY, scale=gs_sb[:, t : t + 1])
+            gy.append(gy_t)
+
+        def half_list(lst, h):
+            return lst[:, h * (HALF // 16) : (h + 1) * (HALF // 16)]
+
+        def round_interleave(engine_copy, dst, src, lo, hi):
+            engine_copy(
+                dst[:, lo:hi, :].rearrange("p (c i) t -> p c t i", i=4),
+                src[:, :, lo:hi].rearrange("p t (c i) -> p c t i", i=4),
+            )
+
+        def round_and_quantise(src, h, words, scales, name):
+            rounded = tile([P, HALF, PACK], BF16, name)
+            if h == 0:
+                round_interleave(nc.scalar.copy, rounded, src, 0, HALF)
+            else:
+                round_interleave(nc.vector.tensor_copy, rounded, src, 0, VCOLS)
+                round_interleave(nc.scalar.copy, rounded, src, VCOLS, HALF)
+            cols = slice(h * HALF, (h + 1) * HALF)
+            return lambda: nc.vector.quantize_mx(
+                out=words[:, cols].bitcast(FP8X4), scales=scales[:, cols], in_=rounded[:].rearrange("p c t -> p (c t)")
+            )
+
+        z_words = tile([P, S], U32, "z_words")
+        z_scales = tile([P, S], U8, "z_scales")
+        z = [tile([P, PACK, HALF], F32, f"z{h}") for h in range(2)]
+        steps = [(h, t) for h in range(2) for t in range(PACK)]
+        second = {}
+        quant = {}
+
+        def z_first(h, t):
+            part = tile([P, HALF], F32, f"zpart{h}{t}")
+            nc.vector.tensor_scalar(part[:], gy[t][:].indirect(half_list(n2_sb, h)), 0.75, 0.0, MULT, ADD)
+            second[h, t] = part
+
+        def z_second(h, t):
+            nc.vector.tensor_tensor(z[h][:, t, :], gy[t][:].indirect(half_list(n1_sb, h)), second[h, t][:], ADD)
+            if t == PACK - 1:
+                quant[h] = round_and_quantise(z[h], h, z_words, z_scales, f"z_bf{h}")
+
+        z_first(*steps[0])
+        for i in range(1, len(steps)):
+            z_first(*steps[i])
+            z_second(*steps[i - 1])
+        quant[0]()
+        z_second(*steps[-1])
+        quant[1]()
+
+        ds = [tile([P, S], F32, f"ds{t}") for t in range(PACK)]
+        for t in range(PACK):
+            for h in range(2):
+                cols = slice(h * HALF, (h + 1) * HALF)
+                acc = psum.tile([P, HALF], F32, name=f"acc_s{t}{h}", tag=f"bank{PACK * (1 - h) + t}")
+                nc.tensor.matmul_mx(
+                    out=acc[:],
+                    lhsT=cwd[:, P * t : P * (t + 1)].bitcast(FP8X4),
+                    lhsT_scale=csd[:, P * t : P * (t + 1)],
+                    rhs=z_words[:, cols].bitcast(FP8X4),
+                    rhs_scale=z_scales[:, cols],
+                    start=True,
+                    stop=True,
+                )
+                nc.scalar.activation(ds[t][:, cols], acc[:], COPY, scale=0.0625)
+
+        pairs = {}
+        neg_half = {}
+
+        def fetch_pairs(t):
+            pa = tile([P, W], F32, f"pa{t}")
+            nc.vector.tensor_copy(pa[:], ds[t][:].indirect(n3_sb[:]))
+            pb = tile([P, W], F32, f"pb{t}")
+            nc.vector.tensor_scalar(pb[:], ds[t][:].indirect(n4_sb[:]), -0.5, 0.0, MULT, ADD)
+            pairs[t] = (pa, pb)
+
+        def put_back(t):
+            pa, pb = pairs[t]
+            nc.vector.tensor_tensor(ds[t][:].indirect(n4_sb[:]), pa[:], pb[:], ADD)
+            neg = tile([P, S], F32, f"neg_half{t}")
+            nc.scalar.activation(neg[:], ds[t][:], COPY, scale=-0.5)
+            neg_half[t] = neg
+
+        fetch_pairs(0)
+        for t in range(1, PACK):
+            fetch_pairs(t)
+            put_back(t - 1)
+        put_back(PACK - 1)
+
+        o_words = tile([P, S], U32, "o_words")
+        o_scales = tile([P, S], U8, "o_scales")
+        out_rows = out_0.rearrange("(p t) j -> p t j", t=PACK)
+        words_out = out_1[0].rearrange("p c r -> p (c r)").bitcast(I32)
+        res = [tile([P, PACK, HALF], F32, f"res{h}") for h in range(2)]
+        oquant = {}
+        for h in range(2):
+            cols = slice(h * HALF, (h + 1) * HALF)
+            for t in range(PACK):
+                if h == 1 and t == PACK - 1:
+                    oquant[0]()
+                    nc.sync.dma_start(out=words_out[:, 0:HALF], in_=o_words[:, 0:HALF].bitcast(I32))
+                nc.vector.tensor_tensor(res[h][:, t, :], neg_half[t][:].indirect(half_list(n5_sb, h)), ds[t][:, cols], ADD)
+                if t % 2 == 1:
+                    nc.sync.dma_start(out=out_rows[:, t - 1 : t + 1, cols], in_=res[h][:, t - 1 : t + 1, :])
+            oquant[h] = round_and_quantise(res[h], h, o_words, o_scales, f"o_bf{h}")
+        oquant[1]()
+        nc.sync.dma_start(out=words_out[:, HALF:S], in_=o_words[:, HALF:S].bitcast(I32))
+        for q in range(4):
+            queue = nc.scalar if q % 2 else nc.sync
+            queue.dma_start(out=out_2[0, 4 * q : 4 * q + 4, :].bitcast(I32), in_=o_scales[32 * q : 32 * q + 4, :].bitcast(I32))

@@ -52,10 +52,10 @@ def tile_picked_candsumfoldd_none_po_kernel(
         offs_sb = load_list(offs, "offs_sb")
         xs = load_scales(x_scales, "xs", nc.sync)
         cand_sb = load_list(cand, "cand_sb")
-        xw = tile([P, T], U32, "xw")
-        nc.sync.dma_start(out=xw[:].bitcast(I32), in_=x_words[0].rearrange("p c r -> p (c r)").bitcast(I32))
         ww = tile([P, 2 * H], U8, "ww")
         nc.sync.dma_start(out=ww[:].bitcast(I32), in_=w1_words[0].bitcast(I32))
+        xw = tile([P, T], U32, "xw")
+        nc.sync.dma_start(out=xw[:].bitcast(I32), in_=x_words[0].rearrange("p c r -> p (c r)").bitcast(I32))
         ws = load_scales(w1_scales, "ws", nc.sync)
         gs_sb = tile([P, PACK], F32, "gs_sb")
         nc.sync.dma_start(out=gs_sb[:], in_=gs.rearrange("(p t) o -> p (t o)", t=PACK))
@@ -68,16 +68,16 @@ def tile_picked_candsumfoldd_none_po_kernel(
         q_scales = tile([P, S], U8, "q_scales")
         nc.vector.tensor_copy(q_scales[:], xs[:].indirect(offs_sb[:]))
         wwd = tile([P, 2 * H], U8, "wwd")
-        nc.vector.tensor_copy(
+        nc.gpsimd.tensor_copy(
             wwd[:].rearrange("p (t m b) -> p t m b", t=PACK, b=2), ww[:].rearrange("p (m t b) -> p t m b", t=PACK, b=2)
         )
         q_words = tile([P, S], U32, "q_words")
         nc.vector.tensor_copy(q_words[:], xw[:].indirect(offs_sb[:]))
         wsd = tile([P, H], U8, "wsd")
-        nc.vector.tensor_copy(wsd[:].rearrange("p (t m) -> p t m", t=PACK), ws[:].rearrange("p (m t) -> p t m", t=PACK))
+        nc.gpsimd.tensor_copy(wsd[:].rearrange("p (t m) -> p t m", t=PACK), ws[:].rearrange("p (m t) -> p t m", t=PACK))
         c_scales = tile([P, C], U8, "c_scales")
         nc.vector.tensor_copy(c_scales[:], xs[:].indirect(cand_sb[:]))
-        c_words = tile([P, C], U32, "c_words", tag="ws")
+        c_words = tile([P, C], U32, "c_words")
         nc.vector.tensor_copy(c_words[:], xw[:].indirect(cand_sb[:]))
         csd = tile([P, C], U8, "csd")
         nc.vector.tensor_copy(csd[:].rearrange("p (t m) -> p t m", t=PACK), c_scales[:].rearrange("p (m t) -> p t m", t=PACK))
@@ -109,13 +109,14 @@ def tile_picked_candsumfoldd_none_po_kernel(
                 src[:, :, lo:hi].rearrange("p t (c i) -> p c t i", i=4),
             )
 
-        def round_and_quantise(src, h, words, scales, name):
+        def round_and_quantise(src, h, words, scales, name, vcols):
             rounded = tile([P, HALF, PACK], BF16, name)
             if h == 0:
                 round_interleave(nc.scalar.copy, rounded, src, 0, HALF)
             else:
-                round_interleave(nc.vector.tensor_copy, rounded, src, 0, VCOLS)
-                round_interleave(nc.scalar.copy, rounded, src, VCOLS, HALF)
+                round_interleave(nc.vector.tensor_copy, rounded, src, 0, vcols)
+                if vcols < HALF:
+                    round_interleave(nc.scalar.copy, rounded, src, vcols, HALF)
             cols = slice(h * HALF, (h + 1) * HALF)
             return lambda: nc.vector.quantize_mx(
                 out=words[:, cols].bitcast(FP8X4), scales=scales[:, cols], in_=rounded[:].rearrange("p c t -> p (c t)")
@@ -123,29 +124,42 @@ def tile_picked_candsumfoldd_none_po_kernel(
 
         z_words = tile([P, S], U32, "z_words")
         z_scales = tile([P, S], U8, "z_scales")
-        z = [tile([P, PACK, HALF], F32, f"z{h}") for h in range(2)]
-        steps = [(h, t) for h in range(2) for t in range(PACK)]
+        z = {0: tile([P, PACK, HALF], F32, "z0", tag="z")}
+        mid_parts = tile([P, 2, 2, HALF], F32, "mid_parts", tag="gs_sb")
         second = {}
         quant = {}
 
         def z_first(h, t):
-            part = tile([P, HALF], F32, f"zpart{h}{t}")
-            nc.vector.tensor_scalar(part[:], gy[t][:].indirect(half_list(n2_sb, h)), 0.75, 0.0, MULT, ADD)
+            part = mid_parts[:, h, t - 1, :] if t in (1, 2) else tile([P, HALF], F32, f"zpart{h}{t}")[:]
+            nc.vector.tensor_scalar(part, gy[t][:].indirect(half_list(n2_sb, h)), 0.75, 0.0, MULT, ADD)
             second[h, t] = part
 
         def z_second(h, t):
-            nc.vector.tensor_tensor(z[h][:, t, :], gy[t][:].indirect(half_list(n1_sb, h)), second[h, t][:], ADD)
+            nc.vector.tensor_tensor(z[h][:, t, :], gy[t][:].indirect(half_list(n1_sb, h)), second[h, t], ADD)
             if t == PACK - 1:
-                quant[h] = round_and_quantise(z[h], h, z_words, z_scales, f"z_bf{h}")
+                quant[h] = round_and_quantise(z[h], h, z_words, z_scales, f"z_bf{h}", VCOLS)
 
-        z_first(*steps[0])
-        for i in range(1, len(steps)):
-            z_first(*steps[i])
-            z_second(*steps[i - 1])
+        z_first(0, 0)
+        z_first(1, 0)
+        z_second(0, 0)
+        z_first(0, 1)
+        z_first(0, 2)
+        z_second(0, 1)
+        z_first(0, 3)
+        z_second(0, 2)
+        z_second(0, 3)
+        for t in range(1, PACK):
+            z_first(1, t)
         quant[0]()
-        z_second(*steps[-1])
+        z[1] = tile([P, PACK, HALF], F32, "z1", tag="z")
+        for t in range(PACK):
+            z_second(1, t)
         quant[1]()
 
+        sixteenth = tile([P, 1], F32, "sixteenth")
+        nc.gpsimd.memset(sixteenth[:], 0.0625)
+        minus_half = tile([P, 1], F32, "minus_half")
+        nc.gpsimd.memset(minus_half[:], -0.5)
         ds = [tile([P, S], F32, f"ds{t}") for t in range(PACK)]
         for t in range(PACK):
             for h in range(2):
@@ -160,27 +174,30 @@ def tile_picked_candsumfoldd_none_po_kernel(
                     start=True,
                     stop=True,
                 )
-                nc.scalar.activation(ds[t][:, cols], acc[:], COPY, scale=0.0625)
+                nc.scalar.activation(ds[t][:, cols], acc[:], COPY, scale=sixteenth[:])
 
+        mid_pairs = tile([P, 2, 2, W], F32, "mid_pairs", tag="sixteenth")
         pairs = {}
         neg_half = {}
 
         def fetch_pairs(t):
-            pa = tile([P, W], F32, f"pa{t}")
-            nc.vector.tensor_copy(pa[:], ds[t][:].indirect(n3_sb[:]))
-            pb = tile([P, W], F32, f"pb{t}")
-            nc.vector.tensor_scalar(pb[:], ds[t][:].indirect(n4_sb[:]), -0.5, 0.0, MULT, ADD)
+            both = mid_pairs[:, t - 1] if t in (1, 2) else tile([P, 2, W], F32, f"pair{t}")[:]
+            pa, pb = both[:, 0, :], both[:, 1, :]
+            nc.vector.tensor_copy(pa, ds[t][:].indirect(n3_sb[:]))
+            nc.vector.tensor_scalar(pb, ds[t][:].indirect(n4_sb[:]), -0.5, 0.0, MULT, ADD)
             pairs[t] = (pa, pb)
 
         def put_back(t):
             pa, pb = pairs[t]
-            nc.vector.tensor_tensor(ds[t][:].indirect(n4_sb[:]), pa[:], pb[:], ADD)
+            nc.vector.tensor_tensor(ds[t][:].indirect(n4_sb[:]), pa, pb, ADD)
             neg = tile([P, S], F32, f"neg_half{t}")
-            nc.scalar.activation(neg[:], ds[t][:], COPY, scale=-0.5)
+            nc.scalar.activation(neg[:], ds[t][:], COPY, scale=minus_half[:])
             neg_half[t] = neg
 
         fetch_pairs(0)
-        for t in range(1, PACK):
+        put_back(0)
+        fetch_pairs(1)
+        for t in range(2, PACK):
             fetch_pairs(t)
             put_back(t - 1)
         put_back(PACK - 1)
@@ -189,18 +206,18 @@ def tile_picked_candsumfoldd_none_po_kernel(
         o_scales = tile([P, S], U8, "o_scales")
         out_rows = out_0.rearrange("(p t) j -> p t j", t=PACK)
         words_out = out_1[0].rearrange("p c r -> p (c r)").bitcast(I32)
-        res = [tile([P, PACK, HALF], F32, f"res{h}") for h in range(2)]
+        res = [tile([P, PACK, HALF], F32, "res0"), tile([P, PACK, HALF], F32, "res1", tag="minus_half")]
         oquant = {}
         for h in range(2):
             cols = slice(h * HALF, (h + 1) * HALF)
             for t in range(PACK):
-                if h == 1 and t == PACK - 1:
-                    oquant[0]()
-                    nc.sync.dma_start(out=words_out[:, 0:HALF], in_=o_words[:, 0:HALF].bitcast(I32))
                 nc.vector.tensor_tensor(res[h][:, t, :], neg_half[t][:].indirect(half_list(n5_sb, h)), ds[t][:, cols], ADD)
                 if t % 2 == 1:
                     nc.sync.dma_start(out=out_rows[:, t - 1 : t + 1, cols], in_=res[h][:, t - 1 : t + 1, :])
-            oquant[h] = round_and_quantise(res[h], h, o_words, o_scales, f"o_bf{h}")
+            if h == 1:
+                oquant[0]()
+                nc.sync.dma_start(out=words_out[:, 0:HALF], in_=o_words[:, 0:HALF].bitcast(I32))
+            oquant[h] = round_and_quantise(res[h], h, o_words, o_scales, f"o_bf{h}", VCOLS)
         oquant[1]()
         nc.sync.dma_start(out=words_out[:, HALF:S], in_=o_words[:, HALF:S].bitcast(I32))
         for q in range(4):

@@ -20,6 +20,7 @@ COPY = mybir.ActivationFunctionType.Copy
 P = 128
 PACK = 4
 HALF = S // 2
+QUARTER = S // 4
 VCOLS = 160
 
 
@@ -100,64 +101,62 @@ def tile_picked_candsumfoldd_none_po_kernel(
             nc.scalar.activation(gy_t[:], acc[:], COPY, scale=gs_sb[:, t : t + 1])
             gy.append(gy_t)
 
-        def half_list(lst, h):
-            return lst[:, h * (HALF // 16) : (h + 1) * (HALF // 16)]
+        def entries(lst, lo, width):
+            return lst[:, lo // 16 : (lo + width) // 16]
 
-        def round_interleave(engine_copy, dst, src, lo, hi):
-            engine_copy(
-                dst[:, lo:hi, :].rearrange("p (c i) t -> p c t i", i=4),
-                src[:, :, lo:hi].rearrange("p t (c i) -> p c t i", i=4),
+        def round_interleave(copy, src, name):
+            width = src.shape[2]
+            rounded = tile([P, width, PACK], BF16, name)
+            copy(
+                rounded[:].rearrange("p (c i) t -> p c t i", i=4),
+                src.rearrange("p t (c i) -> p c t i", i=4),
             )
+            return rounded[:]
 
-        def round_and_quantise(src, h, words, scales, name, vcols):
-            rounded = tile([P, HALF, PACK], BF16, name)
-            if h == 0:
-                round_interleave(nc.scalar.copy, rounded, src, 0, HALF)
-            else:
-                round_interleave(nc.vector.tensor_copy, rounded, src, 0, vcols)
-                if vcols < HALF:
-                    round_interleave(nc.scalar.copy, rounded, src, vcols, HALF)
-            cols = slice(h * HALF, (h + 1) * HALF)
-            return lambda: nc.vector.quantize_mx(
-                out=words[:, cols].bitcast(FP8X4), scales=scales[:, cols], in_=rounded[:].rearrange("p c t -> p (c t)")
+        def quantise(rounded, words, scales, lo):
+            cols = slice(lo, lo + rounded.shape[1])
+            nc.vector.quantize_mx(
+                out=words[:, cols].bitcast(FP8X4), scales=scales[:, cols], in_=rounded.rearrange("p c t -> p (c t)")
             )
 
         z_words = tile([P, S], U32, "z_words")
         z_scales = tile([P, S], U8, "z_scales")
-        z = {0: tile([P, PACK, HALF], F32, "z0", tag="z")}
+        z_left = tile([P, PACK, HALF], F32, "z_left")
         mid_parts = tile([P, 2, 2, HALF], F32, "mid_parts", tag="gs_sb")
         second = {}
-        quant = {}
 
         def z_first(h, t):
             part = mid_parts[:, h, t - 1, :] if t in (1, 2) else tile([P, HALF], F32, f"zpart{h}{t}")[:]
-            nc.vector.tensor_scalar(part, gy[t][:].indirect(half_list(n2_sb, h)), 0.75, 0.0, MULT, ADD)
+            nc.vector.tensor_scalar(part, gy[t][:].indirect(entries(n2_sb, h * HALF, HALF)), 0.75, 0.0, MULT, ADD)
             second[h, t] = part
 
-        def z_second(h, t):
-            nc.vector.tensor_tensor(z[h][:, t, :], gy[t][:].indirect(half_list(n1_sb, h)), second[h, t], ADD)
-            if t == PACK - 1:
-                quant[h] = round_and_quantise(z[h], h, z_words, z_scales, f"z_bf{h}", VCOLS)
+        def z_second(dst, t, lo):
+            width = dst.shape[1]
+            part = second[lo // HALF, t][:, lo % HALF : lo % HALF + width]
+            nc.vector.tensor_tensor(dst, gy[t][:].indirect(entries(n1_sb, lo, width)), part, ADD)
 
         z_first(0, 0)
         z_first(1, 0)
-        z_second(0, 0)
+        z_second(z_left[:, 0, :], 0, 0)
         z_first(0, 1)
-        z_first(0, 2)
-        z_second(0, 1)
-        z_first(0, 3)
-        z_second(0, 2)
-        z_second(0, 3)
+        for t in range(1, PACK):
+            if t + 1 < PACK:
+                z_first(0, t + 1)
+            z_second(z_left[:, t, :], t, 0)
+        left_rounded = round_interleave(nc.scalar.copy, z_left[:], "z_left_bf")
         for t in range(1, PACK):
             z_first(1, t)
-        quant[0]()
-        z[1] = tile([P, PACK, HALF], F32, "z1", tag="z")
-        for t in range(PACK):
-            z_second(1, t)
-        quant[1]()
+        quantise(left_rounded, z_words, z_scales, 0)
+        z_right = tile([P, 2, PACK, QUARTER], F32, "z_right", tag="z_left")
+        for u in range(2):
+            for t in range(PACK):
+                z_second(z_right[:, u, t, :], t, HALF + u * QUARTER)
+        for u, copy in enumerate((nc.scalar.copy, nc.vector.tensor_copy)):
+            quantise(round_interleave(copy, z_right[:, u], f"z_right_bf{u}"), z_words, z_scales, HALF + u * QUARTER)
 
-        sixteenth = tile([P, 1], F32, "sixteenth")
-        nc.gpsimd.memset(sixteenth[:], 0.0625)
+        sixteenth = [tile([P, 1], F32, f"sixteenth{u}") for u in range(2)]
+        for const in sixteenth:
+            nc.gpsimd.memset(const[:], 0.0625)
         minus_half = tile([P, 1], F32, "minus_half")
         nc.gpsimd.memset(minus_half[:], -0.5)
         ds = [tile([P, S], F32, f"ds{t}") for t in range(PACK)]
@@ -165,27 +164,35 @@ def tile_picked_candsumfoldd_none_po_kernel(
             for h in range(2):
                 cols = slice(h * HALF, (h + 1) * HALF)
                 acc = psum.tile([P, HALF], F32, name=f"acc_s{t}{h}", tag=f"bank{PACK * (1 - h) + t}")
-                nc.tensor.matmul_mx(
-                    out=acc[:],
-                    lhsT=cwd[:, P * t : P * (t + 1)].bitcast(FP8X4),
-                    lhsT_scale=csd[:, P * t : P * (t + 1)],
-                    rhs=z_words[:, cols].bitcast(FP8X4),
-                    rhs_scale=z_scales[:, cols],
-                    start=True,
-                    stop=True,
-                )
-                nc.scalar.activation(ds[t][:, cols], acc[:], COPY, scale=sixteenth[:])
+                width = QUARTER if h else HALF
+                for lo in range(0, HALF, width):
+                    rhs_cols = slice(h * HALF + lo, h * HALF + lo + width)
+                    nc.tensor.matmul_mx(
+                        out=acc[:, lo : lo + width],
+                        lhsT=cwd[:, P * t : P * (t + 1)].bitcast(FP8X4),
+                        lhsT_scale=csd[:, P * t : P * (t + 1)],
+                        rhs=z_words[:, rhs_cols].bitcast(FP8X4),
+                        rhs_scale=z_scales[:, rhs_cols],
+                        start=True,
+                        stop=True,
+                    )
+                nc.scalar.activation(ds[t][:, cols], acc[:], COPY, scale=sixteenth[t // 2][:])
 
-        mid_pairs = tile([P, 2, 2, W], F32, "mid_pairs", tag="sixteenth")
-        pairs = {}
+        pa_first = tile([P, W], F32, "pa_first")
+        early = tile([P, 3, W], F32, "early", tag="sixteenth0")
+        late = tile([P, 2, 2, W], F32, "late", tag="sixteenth1")
+        pairs = {
+            0: (pa_first[:], early[:, 0, :]),
+            1: (early[:, 1, :], early[:, 2, :]),
+            2: (late[:, 0, 0, :], late[:, 0, 1, :]),
+            3: (late[:, 1, 0, :], late[:, 1, 1, :]),
+        }
         neg_half = {}
 
         def fetch_pairs(t):
-            both = mid_pairs[:, t - 1] if t in (1, 2) else tile([P, 2, W], F32, f"pair{t}")[:]
-            pa, pb = both[:, 0, :], both[:, 1, :]
+            pa, pb = pairs[t]
             nc.vector.tensor_copy(pa, ds[t][:].indirect(n3_sb[:]))
             nc.vector.tensor_scalar(pb, ds[t][:].indirect(n4_sb[:]), -0.5, 0.0, MULT, ADD)
-            pairs[t] = (pa, pb)
 
         def put_back(t):
             pa, pb = pairs[t]
@@ -195,9 +202,7 @@ def tile_picked_candsumfoldd_none_po_kernel(
             neg_half[t] = neg
 
         fetch_pairs(0)
-        put_back(0)
-        fetch_pairs(1)
-        for t in range(2, PACK):
+        for t in range(1, PACK):
             fetch_pairs(t)
             put_back(t - 1)
         put_back(PACK - 1)
@@ -206,19 +211,32 @@ def tile_picked_candsumfoldd_none_po_kernel(
         o_scales = tile([P, S], U8, "o_scales")
         out_rows = out_0.rearrange("(p t) j -> p t j", t=PACK)
         words_out = out_1[0].rearrange("p c r -> p (c r)").bitcast(I32)
-        res = [tile([P, PACK, HALF], F32, "res0"), tile([P, PACK, HALF], F32, "res1", tag="minus_half")]
-        oquant = {}
-        for h in range(2):
-            cols = slice(h * HALF, (h + 1) * HALF)
-            for t in range(PACK):
-                nc.vector.tensor_tensor(res[h][:, t, :], neg_half[t][:].indirect(half_list(n5_sb, h)), ds[t][:, cols], ADD)
-                if t % 2 == 1:
-                    nc.sync.dma_start(out=out_rows[:, t - 1 : t + 1, cols], in_=res[h][:, t - 1 : t + 1, :])
-            if h == 1:
-                oquant[0]()
-                nc.sync.dma_start(out=words_out[:, 0:HALF], in_=o_words[:, 0:HALF].bitcast(I32))
-            oquant[h] = round_and_quantise(res[h], h, o_words, o_scales, f"o_bf{h}", VCOLS)
-        oquant[1]()
+
+        def finish(dst, t, lo):
+            width = dst.shape[1]
+            nc.vector.tensor_tensor(dst, neg_half[t][:].indirect(entries(n5_sb, lo, width)), ds[t][:, lo : lo + width], ADD)
+
+        res_left = tile([P, PACK, HALF], F32, "res_left")
+        for t in range(PACK):
+            finish(res_left[:, t, :], t, 0)
+            if t % 2 == 1:
+                nc.sync.dma_start(out=out_rows[:, t - 1 : t + 1, 0:HALF], in_=res_left[:, t - 1 : t + 1, :])
+        left_rounded = round_interleave(nc.scalar.copy, res_left[:], "res_left_bf")
+        res_right = tile([P, PACK, HALF], F32, "res_right", tag="minus_half")
+        for t in range(PACK):
+            finish(res_right[:, t, :], t, HALF)
+            if t % 2 == 1:
+                nc.sync.dma_start(out=out_rows[:, t - 1 : t + 1, HALF:S], in_=res_right[:, t - 1 : t + 1, :])
+        quantise(left_rounded[:, 0:QUARTER, :], o_words, o_scales, 0)
+        right_rounded = tile([P, HALF, PACK], BF16, "res_right_bf")
+        for copy, lo, hi in ((nc.vector.tensor_copy, 0, VCOLS), (nc.scalar.copy, VCOLS, HALF)):
+            copy(
+                right_rounded[:, lo:hi, :].rearrange("p (c i) t -> p c t i", i=4),
+                res_right[:, :, lo:hi].rearrange("p t (c i) -> p c t i", i=4),
+            )
+        quantise(left_rounded[:, QUARTER:HALF, :], o_words, o_scales, QUARTER)
+        nc.sync.dma_start(out=words_out[:, 0:HALF], in_=o_words[:, 0:HALF].bitcast(I32))
+        quantise(right_rounded[:], o_words, o_scales, HALF)
         nc.sync.dma_start(out=words_out[:, HALF:S], in_=o_words[:, HALF:S].bitcast(I32))
         for q in range(4):
             queue = nc.scalar if q % 2 else nc.sync

@@ -19,9 +19,12 @@ COPY = mybir.ActivationFunctionType.Copy
 
 P = 128
 PACK = 4
+QUADRANTS, QUADRANT = 4, 32
+GROUP = 16
+RUN = 4
 HALF = S // 2
 QUARTER = S // 4
-VCOLS = 160
+VECTOR_COLS = 160
 
 
 def tile_picked_candsumfoldd_none_po_kernel(
@@ -40,77 +43,27 @@ def tile_picked_candsumfoldd_none_po_kernel(
             nc.sync.dma_start(lst[:], src)
             return lst
 
-        def load_scales(src, name, queue):
-            width = src.shape[2]
-            plane = tile([P, width], U8, name)
-            for q in range(4):
-                queue.dma_start(
-                    out=plane[32 * q : 32 * q + 32, :].bitcast(I32),
-                    in_=src[0, 4 * q : 4 * q + 4, :].bitcast(I32).partition_broadcast(8),
+        def load_scales(src, name):
+            plane = tile([P, src.shape[2]], U8, name)
+            for q in range(QUADRANTS):
+                nc.sync.dma_start(
+                    out=plane[QUADRANT * q : QUADRANT * (q + 1), :].bitcast(I32),
+                    in_=src[0, PACK * q : PACK * (q + 1), :].bitcast(I32).partition_broadcast(QUADRANT // PACK),
                 )
             return plane
 
-        offs_sb = load_list(offs, "offs_sb")
-        xs = load_scales(x_scales, "xs", nc.sync)
-        cand_sb = load_list(cand, "cand_sb")
-        ww = tile([P, 2 * H], U8, "ww")
-        nc.sync.dma_start(out=ww[:].bitcast(I32), in_=w1_words[0].bitcast(I32))
-        xw = tile([P, T], U32, "xw")
-        nc.sync.dma_start(out=xw[:].bitcast(I32), in_=x_words[0].rearrange("p c r -> p (c r)").bitcast(I32))
-        ws = load_scales(w1_scales, "ws", nc.sync)
-        gs_sb = tile([P, PACK], F32, "gs_sb")
-        nc.sync.dma_start(out=gs_sb[:], in_=gs.rearrange("(p t) o -> p (t o)", t=PACK))
-        n1_sb = load_list(n1, "n1_sb")
-        n2_sb = load_list(n2, "n2_sb")
-        n3_sb = load_list(n3, "n3_sb")
-        n4_sb = load_list(n4, "n4_sb")
-        n5_sb = load_list(n5, "n5_sb")
-
-        q_scales = tile([P, S], U8, "q_scales")
-        nc.vector.tensor_copy(q_scales[:], xs[:].indirect(offs_sb[:]))
-        wwd = tile([P, 2 * H], U8, "wwd")
-        nc.gpsimd.tensor_copy(
-            wwd[:].rearrange("p (t m b) -> p t m b", t=PACK, b=2), ww[:].rearrange("p (m t b) -> p t m b", t=PACK, b=2)
-        )
-        q_words = tile([P, S], U32, "q_words")
-        nc.vector.tensor_copy(q_words[:], xw[:].indirect(offs_sb[:]))
-        wsd = tile([P, H], U8, "wsd")
-        nc.gpsimd.tensor_copy(wsd[:].rearrange("p (t m) -> p t m", t=PACK), ws[:].rearrange("p (m t) -> p t m", t=PACK))
-        c_scales = tile([P, C], U8, "c_scales")
-        nc.vector.tensor_copy(c_scales[:], xs[:].indirect(cand_sb[:]))
-        c_words = tile([P, C], U32, "c_words")
-        nc.vector.tensor_copy(c_words[:], xw[:].indirect(cand_sb[:]))
-        csd = tile([P, C], U8, "csd")
-        nc.vector.tensor_copy(csd[:].rearrange("p (t m) -> p t m", t=PACK), c_scales[:].rearrange("p (m t) -> p t m", t=PACK))
-        cwd = tile([P, C], U32, "cwd")
-        nc.vector.tensor_copy(cwd[:].rearrange("p (t m) -> p m t", t=PACK), c_words[:].rearrange("p (m t) -> p m t", t=PACK))
-
-        gy = []
-        for t in range(PACK):
-            acc = psum.tile([P, S], F32, name=f"acc_y{t}", tag=f"bank{t}")
-            nc.tensor.matmul_mx(
-                out=acc[:],
-                lhsT=wwd[:, 2 * P * t : 2 * P * (t + 1)].bitcast(FP4X4),
-                lhsT_scale=wsd[:, P * t : P * (t + 1)],
-                rhs=q_words[:].bitcast(FP8X4),
-                rhs_scale=q_scales[:],
-                start=True,
-                stop=True,
-            )
-            gy_t = tile([P, S], F32, f"gy{t}")
-            nc.scalar.activation(gy_t[:], acc[:], COPY, scale=gs_sb[:, t : t + 1])
-            gy.append(gy_t)
-
         def entries(lst, lo, width):
-            return lst[:, lo // 16 : (lo + width) // 16]
+            return lst[:, lo // GROUP : (lo + width) // GROUP]
 
-        def round_interleave(copy, src, name):
-            width = src.shape[2]
-            rounded = tile([P, width, PACK], BF16, name)
+        def round_columns(copy, rounded, values):
             copy(
-                rounded[:].rearrange("p (c i) t -> p c t i", i=4),
-                src.rearrange("p t (c i) -> p c t i", i=4),
+                rounded.rearrange("p (c i) t -> p c t i", i=RUN),
+                values.rearrange("p t (c i) -> p c t i", i=RUN),
             )
+
+        def round_all(copy, values, name):
+            rounded = tile([P, values.shape[2], PACK], BF16, name)
+            round_columns(copy, rounded[:], values)
             return rounded[:]
 
         def quantise(rounded, words, scales, lo):
@@ -119,77 +72,140 @@ def tile_picked_candsumfoldd_none_po_kernel(
                 out=words[:, cols].bitcast(FP8X4), scales=scales[:, cols], in_=rounded.rearrange("p c t -> p (c t)")
             )
 
+        offs_sb = load_list(offs, "offs_sb")
+        x_plane = load_scales(x_scales, "x_plane")
+        cand_sb = load_list(cand, "cand_sb")
+        w_codes = tile([P, 2 * H], U8, "w_codes")
+        nc.sync.dma_start(out=w_codes[:].bitcast(I32), in_=w1_words[0].bitcast(I32))
+        x_codes = tile([P, T], U32, "x_codes")
+        nc.sync.dma_start(out=x_codes[:].bitcast(I32), in_=x_words[0].rearrange("p c r -> p (c r)").bitcast(I32))
+        w_plane = load_scales(w1_scales, "w_plane")
+        gs_sb = tile([P, PACK], F32, "gs_sb")
+        nc.sync.dma_start(out=gs_sb[:], in_=gs.rearrange("(p t) o -> p (t o)", t=PACK))
+        n1_sb = load_list(n1, "n1_sb")
+        n2_sb = load_list(n2, "n2_sb")
+        n3_sb = load_list(n3, "n3_sb")
+        n4_sb = load_list(n4, "n4_sb")
+        n5_sb = load_list(n5, "n5_sb")
+
+        picked_scales = tile([P, S], U8, "picked_scales")
+        nc.vector.tensor_copy(picked_scales[:], x_plane[:].indirect(offs_sb[:]))
+        w_dealt = tile([P, 2 * H], U8, "w_dealt")
+        nc.gpsimd.tensor_copy(
+            w_dealt[:].rearrange("p (t m b) -> p t m b", t=PACK, b=2),
+            w_codes[:].rearrange("p (m t b) -> p t m b", t=PACK, b=2),
+        )
+        picked_words = tile([P, S], U32, "picked_words")
+        nc.vector.tensor_copy(picked_words[:], x_codes[:].indirect(offs_sb[:]))
+        w_scales_dealt = tile([P, H], U8, "w_scales_dealt")
+        nc.gpsimd.tensor_copy(
+            w_scales_dealt[:].rearrange("p (t m) -> p t m", t=PACK), w_plane[:].rearrange("p (m t) -> p t m", t=PACK)
+        )
+        cand_scales = tile([P, C], U8, "cand_scales")
+        nc.vector.tensor_copy(cand_scales[:], x_plane[:].indirect(cand_sb[:]))
+        cand_words = tile([P, C], U32, "cand_words")
+        nc.vector.tensor_copy(cand_words[:], x_codes[:].indirect(cand_sb[:]))
+        cand_scales_dealt = tile([P, C], U8, "cand_scales_dealt", tag="w_plane")
+        nc.vector.tensor_copy(
+            cand_scales_dealt[:].rearrange("p (t m) -> p t m", t=PACK),
+            cand_scales[:].rearrange("p (m t) -> p t m", t=PACK),
+        )
+        cand_dealt = tile([P, C], U32, "cand_dealt")
+        nc.vector.tensor_copy(
+            cand_dealt[:].rearrange("p (t m) -> p m t", t=PACK), cand_words[:].rearrange("p (m t) -> p m t", t=PACK)
+        )
+
+        gy = []
+        for t in range(PACK):
+            acc = psum.tile([P, S], F32, name=f"acc_y{t}", tag=f"bank{t}")
+            nc.tensor.matmul_mx(
+                out=acc[:],
+                lhsT=w_dealt[:, 2 * P * t : 2 * P * (t + 1)].bitcast(FP4X4),
+                lhsT_scale=w_scales_dealt[:, P * t : P * (t + 1)],
+                rhs=picked_words[:].bitcast(FP8X4),
+                rhs_scale=picked_scales[:],
+                start=True,
+                stop=True,
+            )
+            gy_t = tile([P, S], F32, f"gy{t}")
+            nc.scalar.activation(gy_t[:], acc[:], COPY, scale=gs_sb[:, t : t + 1])
+            gy.append(gy_t)
+
         z_words = tile([P, S], U32, "z_words")
         z_scales = tile([P, S], U8, "z_scales")
         z_left = tile([P, PACK, HALF], F32, "z_left")
-        mid_parts = tile([P, 2, 2, HALF], F32, "mid_parts", tag="gs_sb")
-        second = {}
+        mid_terms = tile([P, 2, 2, HALF], F32, "mid_terms", tag="gs_sb")
+        terms = {}
 
-        def z_first(h, t):
-            part = mid_parts[:, h, t - 1, :] if t in (1, 2) else tile([P, HALF], F32, f"zpart{h}{t}")[:]
-            nc.vector.tensor_scalar(part, gy[t][:].indirect(entries(n2_sb, h * HALF, HALF)), 0.75, 0.0, MULT, ADD)
-            second[h, t] = part
+        def n2_term(h, t):
+            term = mid_terms[:, h, t - 1, :] if t in (1, 2) else tile([P, HALF], F32, f"term{h}{t}")[:]
+            nc.vector.tensor_scalar(term, gy[t][:].indirect(entries(n2_sb, h * HALF, HALF)), 0.75, 0.0, MULT, ADD)
+            terms[h, t] = term
 
-        def z_second(dst, t, lo):
+        def add_n1_term(dst, t, lo):
             width = dst.shape[1]
-            part = second[lo // HALF, t][:, lo % HALF : lo % HALF + width]
-            nc.vector.tensor_tensor(dst, gy[t][:].indirect(entries(n1_sb, lo, width)), part, ADD)
+            term = terms[lo // HALF, t][:, lo % HALF : lo % HALF + width]
+            nc.vector.tensor_tensor(dst, gy[t][:].indirect(entries(n1_sb, lo, width)), term, ADD)
 
-        z_first(0, 0)
-        z_first(1, 0)
-        z_second(z_left[:, 0, :], 0, 0)
-        z_first(0, 1)
+        n2_term(0, 0)
+        n2_term(1, 0)
+        add_n1_term(z_left[:, 0, :], 0, 0)
+        n2_term(0, 1)
         for t in range(1, PACK):
             if t + 1 < PACK:
-                z_first(0, t + 1)
-            z_second(z_left[:, t, :], t, 0)
-        left_rounded = round_interleave(nc.scalar.copy, z_left[:], "z_left_bf")
+                n2_term(0, t + 1)
+            add_n1_term(z_left[:, t, :], t, 0)
+        z_left_rounded = round_all(nc.scalar.copy, z_left[:], "z_left_rounded")
         for t in range(1, PACK):
-            z_first(1, t)
-        quantise(left_rounded, z_words, z_scales, 0)
+            n2_term(1, t)
+        quantise(z_left_rounded, z_words, z_scales, 0)
         z_right = tile([P, 2, PACK, QUARTER], F32, "z_right", tag="z_left")
         for u in range(2):
             for t in range(PACK):
-                z_second(z_right[:, u, t, :], t, HALF + u * QUARTER)
+                add_n1_term(z_right[:, u, t, :], t, HALF + u * QUARTER)
         for u, copy in enumerate((nc.scalar.copy, nc.vector.tensor_copy)):
-            quantise(round_interleave(copy, z_right[:, u], f"z_right_bf{u}"), z_words, z_scales, HALF + u * QUARTER)
+            quantise(round_all(copy, z_right[:, u], f"z_right_rounded{u}"), z_words, z_scales, HALF + u * QUARTER)
 
         sixteenth = [tile([P, 1], F32, f"sixteenth{u}") for u in range(2)]
-        for const in sixteenth:
-            nc.gpsimd.memset(const[:], 0.0625)
+        for factor in sixteenth:
+            nc.gpsimd.memset(factor[:], 0.0625)
         minus_half = tile([P, 1], F32, "minus_half")
         nc.gpsimd.memset(minus_half[:], -0.5)
         ds = [tile([P, S], F32, f"ds{t}") for t in range(PACK)]
+
+        def scores(t, lo, width, bank):
+            cols = slice(lo, lo + width)
+            acc = psum.tile([P, width], F32, name=f"acc_s{t}_{lo}", tag=f"bank{bank}")
+            nc.tensor.matmul_mx(
+                out=acc[:],
+                lhsT=cand_dealt[:, P * t : P * (t + 1)].bitcast(FP8X4),
+                lhsT_scale=cand_scales_dealt[:, P * t : P * (t + 1)],
+                rhs=z_words[:, cols].bitcast(FP8X4),
+                rhs_scale=z_scales[:, cols],
+                start=True,
+                stop=True,
+            )
+            nc.scalar.activation(ds[t][:, cols], acc[:], COPY, scale=sixteenth[t // 2][:])
+
         for t in range(PACK):
-            for h in range(2):
-                cols = slice(h * HALF, (h + 1) * HALF)
-                acc = psum.tile([P, HALF], F32, name=f"acc_s{t}{h}", tag=f"bank{PACK * (1 - h) + t}")
-                width = QUARTER if h else HALF
-                for lo in range(0, HALF, width):
-                    rhs_cols = slice(h * HALF + lo, h * HALF + lo + width)
-                    nc.tensor.matmul_mx(
-                        out=acc[:, lo : lo + width],
-                        lhsT=cwd[:, P * t : P * (t + 1)].bitcast(FP8X4),
-                        lhsT_scale=csd[:, P * t : P * (t + 1)],
-                        rhs=z_words[:, rhs_cols].bitcast(FP8X4),
-                        rhs_scale=z_scales[:, rhs_cols],
-                        start=True,
-                        stop=True,
-                    )
-                nc.scalar.activation(ds[t][:, cols], acc[:], COPY, scale=sixteenth[t // 2][:])
+            scores(t, 0, HALF, PACK + t)
+        scores(0, HALF, QUARTER, 0)
+        scores(0, HALF + QUARTER, QUARTER, PACK)
+        for t in range(1, PACK):
+            scores(t, HALF, HALF, t)
 
         pa_first = tile([P, W], F32, "pa_first")
         early = tile([P, 3, W], F32, "early", tag="sixteenth0")
         late = tile([P, 2, 2, W], F32, "late", tag="sixteenth1")
-        pairs = {
-            0: (pa_first[:], early[:, 0, :]),
-            1: (early[:, 1, :], early[:, 2, :]),
-            2: (late[:, 0, 0, :], late[:, 0, 1, :]),
-            3: (late[:, 1, 0, :], late[:, 1, 1, :]),
-        }
-        neg_half = {}
+        pairs = [
+            (pa_first[:], early[:, 0, :]),
+            (early[:, 1, :], early[:, 2, :]),
+            (late[:, 0, 0, :], late[:, 0, 1, :]),
+            (late[:, 1, 0, :], late[:, 1, 1, :]),
+        ]
+        neg_half_ds = {}
 
-        def fetch_pairs(t):
+        def fetch_pair(t):
             pa, pb = pairs[t]
             nc.vector.tensor_copy(pa, ds[t][:].indirect(n3_sb[:]))
             nc.vector.tensor_scalar(pb, ds[t][:].indirect(n4_sb[:]), -0.5, 0.0, MULT, ADD)
@@ -197,47 +213,53 @@ def tile_picked_candsumfoldd_none_po_kernel(
         def put_back(t):
             pa, pb = pairs[t]
             nc.vector.tensor_tensor(ds[t][:].indirect(n4_sb[:]), pa, pb, ADD)
-            neg = tile([P, S], F32, f"neg_half{t}")
-            nc.scalar.activation(neg[:], ds[t][:], COPY, scale=minus_half[:])
-            neg_half[t] = neg
+            scaled = tile([P, S], F32, f"neg_half_ds{t}")
+            nc.scalar.activation(scaled[:], ds[t][:], COPY, scale=minus_half[:])
+            neg_half_ds[t] = scaled
 
-        fetch_pairs(0)
+        fetch_pair(0)
         for t in range(1, PACK):
-            fetch_pairs(t)
+            fetch_pair(t)
             put_back(t - 1)
         put_back(PACK - 1)
 
-        o_words = tile([P, S], U32, "o_words")
-        o_scales = tile([P, S], U8, "o_scales")
+        out_words = tile([P, S], U32, "out_words")
+        out_scales = tile([P, S], U8, "out_scales")
         out_rows = out_0.rearrange("(p t) j -> p t j", t=PACK)
-        words_out = out_1[0].rearrange("p c r -> p (c r)").bitcast(I32)
+        words_dram = out_1[0].rearrange("p c r -> p (c r)").bitcast(I32)
 
-        def finish(dst, t, lo):
+        def fold(dst, t, lo):
             width = dst.shape[1]
-            nc.vector.tensor_tensor(dst, neg_half[t][:].indirect(entries(n5_sb, lo, width)), ds[t][:, lo : lo + width], ADD)
-
-        res_left = tile([P, PACK, HALF], F32, "res_left")
-        for t in range(PACK):
-            finish(res_left[:, t, :], t, 0)
-            if t % 2 == 1:
-                nc.sync.dma_start(out=out_rows[:, t - 1 : t + 1, 0:HALF], in_=res_left[:, t - 1 : t + 1, :])
-        left_rounded = round_interleave(nc.scalar.copy, res_left[:], "res_left_bf")
-        res_right = tile([P, PACK, HALF], F32, "res_right", tag="minus_half")
-        for t in range(PACK):
-            finish(res_right[:, t, :], t, HALF)
-            if t % 2 == 1:
-                nc.sync.dma_start(out=out_rows[:, t - 1 : t + 1, HALF:S], in_=res_right[:, t - 1 : t + 1, :])
-        quantise(left_rounded[:, 0:QUARTER, :], o_words, o_scales, 0)
-        right_rounded = tile([P, HALF, PACK], BF16, "res_right_bf")
-        for copy, lo, hi in ((nc.vector.tensor_copy, 0, VCOLS), (nc.scalar.copy, VCOLS, HALF)):
-            copy(
-                right_rounded[:, lo:hi, :].rearrange("p (c i) t -> p c t i", i=4),
-                res_right[:, :, lo:hi].rearrange("p t (c i) -> p c t i", i=4),
+            nc.vector.tensor_tensor(
+                dst, neg_half_ds[t][:].indirect(entries(n5_sb, lo, width)), ds[t][:, lo : lo + width], ADD
             )
-        quantise(left_rounded[:, QUARTER:HALF, :], o_words, o_scales, QUARTER)
-        nc.sync.dma_start(out=words_out[:, 0:HALF], in_=o_words[:, 0:HALF].bitcast(I32))
-        quantise(right_rounded[:], o_words, o_scales, HALF)
-        nc.sync.dma_start(out=words_out[:, HALF:S], in_=o_words[:, HALF:S].bitcast(I32))
-        for q in range(4):
+
+        def store_rows(values, first, last, lo):
+            nc.sync.dma_start(out=out_rows[:, first : last + 1, lo : lo + HALF], in_=values[:, first : last + 1, :])
+
+        out_left = tile([P, PACK, HALF], F32, "out_left")
+        for t in range(PACK):
+            fold(out_left[:, t, :], t, 0)
+            if t % 2 == 1:
+                store_rows(out_left, t - 1, t, 0)
+        out_left_rounded = round_all(nc.scalar.copy, out_left[:], "out_left_rounded")
+        out_right = tile([P, PACK, HALF], F32, "out_right", tag="minus_half")
+        for t in range(PACK - 1):
+            fold(out_right[:, t, :], t, HALF)
+        store_rows(out_right, 0, PACK - 2, HALF)
+        fold(out_right[:, PACK - 1, :], PACK - 1, HALF)
+        store_rows(out_right, PACK - 1, PACK - 1, HALF)
+        quantise(out_left_rounded[:, 0:QUARTER, :], out_words, out_scales, 0)
+        out_right_rounded = tile([P, HALF, PACK], BF16, "out_right_rounded")
+        for copy, lo, hi in ((nc.vector.tensor_copy, 0, VECTOR_COLS), (nc.scalar.copy, VECTOR_COLS, HALF)):
+            round_columns(copy, out_right_rounded[:, lo:hi, :], out_right[:, :, lo:hi])
+        quantise(out_left_rounded[:, QUARTER:HALF, :], out_words, out_scales, QUARTER)
+        nc.sync.dma_start(out=words_dram[:, 0:HALF], in_=out_words[:, 0:HALF].bitcast(I32))
+        quantise(out_right_rounded[:], out_words, out_scales, HALF)
+        nc.sync.dma_start(out=words_dram[:, HALF:S], in_=out_words[:, HALF:S].bitcast(I32))
+        for q in range(QUADRANTS):
             queue = nc.scalar if q % 2 else nc.sync
-            queue.dma_start(out=out_2[0, 4 * q : 4 * q + 4, :].bitcast(I32), in_=o_scales[32 * q : 32 * q + 4, :].bitcast(I32))
+            queue.dma_start(
+                out=out_2[0, PACK * q : PACK * (q + 1), :].bitcast(I32),
+                in_=out_scales[QUADRANT * q : QUADRANT * q + PACK, :].bitcast(I32),
+            )

from contextlib import ExitStack

import concourse.mybir as mybir

K, T, S, H, C, W = 512, 2048, 512, 512, 512, 256
FLOPS = 2 * K * H * S + 2 * K * C * S

F32 = mybir.dt.float32
BF16 = mybir.dt.bfloat16
I32 = mybir.dt.int32
U32 = mybir.dt.uint32
U16 = mybir.dt.uint16
U8 = mybir.dt.uint8
FP8X4 = mybir.dt.float8_e4m3fn_x4
FP4X4 = mybir.dt.float4_e2m1fn_x4
MULT = mybir.AluOpType.mult
ADD = mybir.AluOpType.add
COPY = mybir.ActivationFunctionType.Copy

P = 128
PACK = 4
QUADRANTS, QUADRANT = 4, 32
GROUP = 16
RUN = 4
HALF = S // 2
QUARTER = S // 4
VECTOR_COLS = 160


def tile_picked_candsumfoldd_none_po_kernel(
    tc, x_words, x_scales, w1_words, w1_scales, gs, offs, n1, n2, cand, n3, n4, n5, out_0, out_1, out_2
):
    nc = tc.nc
    with ExitStack() as ctx:
        keep = ctx.enter_context(tc.tile_pool(name="keep", bufs=1))
        psum = ctx.enter_context(tc.psum_pool(name="psum", bufs=1))

        def tile(shape, dtype, name, tag=None):
            return keep.tile(shape, dtype, name=name, tag=tag or name, align_bytes=64)

        def load_list(src, name):
            lst = tile([P, src.shape[1]], U16, name)
            nc.sync.dma_start(lst[:], src)
            return lst

        def load_scales(src, name):
            plane = tile([P, src.shape[2]], U8, name)
            for q in range(QUADRANTS):
                nc.sync.dma_start(
                    out=plane[QUADRANT * q : QUADRANT * (q + 1), :].bitcast(I32),
                    in_=src[0, PACK * q : PACK * (q + 1), :].bitcast(I32).partition_broadcast(QUADRANT // PACK),
                )
            return plane

        def entries(lst, lo, width):
            return lst[:, lo // GROUP : (lo + width) // GROUP]

        def round_columns(copy, rounded, values):
            copy(
                rounded.rearrange("p (c i) t -> p c t i", i=RUN),
                values.rearrange("p t (c i) -> p c t i", i=RUN),
            )

        def round_all(copy, values, name):
            rounded = tile([P, values.shape[2], PACK], BF16, name)
            round_columns(copy, rounded[:], values)
            return rounded[:]

        def quantise(rounded, words, scales, lo):
            cols = slice(lo, lo + rounded.shape[1])
            nc.vector.quantize_mx(
                out=words[:, cols].bitcast(FP8X4), scales=scales[:, cols], in_=rounded.rearrange("p c t -> p (c t)")
            )

        offs_sb = load_list(offs, "offs_sb")
        x_plane = load_scales(x_scales, "x_plane")
        cand_sb = load_list(cand, "cand_sb")
        w_codes = tile([P, 2 * H], U8, "w_codes")
        nc.sync.dma_start(out=w_codes[:].bitcast(I32), in_=w1_words[0].bitcast(I32))
        x_codes = tile([P, T], U32, "x_codes")
        nc.sync.dma_start(out=x_codes[:].bitcast(I32), in_=x_words[0].rearrange("p c r -> p (c r)").bitcast(I32))
        w_plane = load_scales(w1_scales, "w_plane")
        gs_sb = tile([P, PACK], F32, "gs_sb")
        nc.sync.dma_start(out=gs_sb[:], in_=gs.rearrange("(p t) o -> p (t o)", t=PACK))
        n1_sb = load_list(n1, "n1_sb")
        n2_sb = load_list(n2, "n2_sb")
        n3_sb = load_list(n3, "n3_sb")
        n4_sb = load_list(n4, "n4_sb")
        n5_sb = load_list(n5, "n5_sb")

        picked_scales = tile([P, S], U8, "picked_scales")
        nc.vector.tensor_copy(picked_scales[:], x_plane[:].indirect(offs_sb[:]))
        w_dealt = tile([P, 2 * H], U8, "w_dealt")
        nc.gpsimd.tensor_copy(
            w_dealt[:].rearrange("p (t m b) -> p t m b", t=PACK, b=2),
            w_codes[:].rearrange("p (m t b) -> p t m b", t=PACK, b=2),
        )
        picked_words = tile([P, S], U32, "picked_words")
        nc.vector.tensor_copy(picked_words[:], x_codes[:].indirect(offs_sb[:]))
        w_scales_dealt = tile([P, H], U8, "w_scales_dealt")
        nc.gpsimd.tensor_copy(
            w_scales_dealt[:].rearrange("p (t m) -> p t m", t=PACK), w_plane[:].rearrange("p (m t) -> p t m", t=PACK)
        )
        cand_scales = tile([P, C], U8, "cand_scales")
        nc.vector.tensor_copy(cand_scales[:], x_plane[:].indirect(cand_sb[:]))
        cand_words = tile([P, C], U32, "cand_words")
        nc.vector.tensor_copy(cand_words[:], x_codes[:].indirect(cand_sb[:]))
        cand_scales_dealt = tile([P, C], U8, "cand_scales_dealt", tag="w_plane")
        nc.vector.tensor_copy(
            cand_scales_dealt[:].rearrange("p (t m) -> p t m", t=PACK),
            cand_scales[:].rearrange("p (m t) -> p t m", t=PACK),
        )
        cand_dealt = tile([P, C], U32, "cand_dealt")
        nc.vector.tensor_copy(
            cand_dealt[:].rearrange("p (t m) -> p m t", t=PACK), cand_words[:].rearrange("p (m t) -> p m t", t=PACK)
        )

        gy = []
        for t in range(PACK):
            acc = psum.tile([P, S], F32, name=f"acc_y{t}", tag=f"bank{t}")
            nc.tensor.matmul_mx(
                out=acc[:],
                lhsT=w_dealt[:, 2 * P * t : 2 * P * (t + 1)].bitcast(FP4X4),
                lhsT_scale=w_scales_dealt[:, P * t : P * (t + 1)],
                rhs=picked_words[:].bitcast(FP8X4),
                rhs_scale=picked_scales[:],
                start=True,
                stop=True,
            )
            gy_t = tile([P, S], F32, f"gy{t}")
            nc.scalar.activation(gy_t[:], acc[:], COPY, scale=gs_sb[:, t : t + 1])
            gy.append(gy_t)

        z_words = tile([P, S], U32, "z_words")
        z_scales = tile([P, S], U8, "z_scales")
        z_left = tile([P, PACK, HALF], F32, "z_left")
        mid_terms = tile([P, 2, 2, HALF], F32, "mid_terms", tag="gs_sb")
        terms = {}

        def n2_term(h, t):
            term = mid_terms[:, h, t - 1, :] if t in (1, 2) else tile([P, HALF], F32, f"term{h}{t}")[:]
            nc.vector.tensor_scalar(term, gy[t][:].indirect(entries(n2_sb, h * HALF, HALF)), 0.75, 0.0, MULT, ADD)
            terms[h, t] = term

        def add_n1_term(dst, t, lo):
            width = dst.shape[1]
            term = terms[lo // HALF, t][:, lo % HALF : lo % HALF + width]
            nc.vector.tensor_tensor(dst, gy[t][:].indirect(entries(n1_sb, lo, width)), term, ADD)

        n2_term(0, 0)
        n2_term(1, 0)
        add_n1_term(z_left[:, 0, :], 0, 0)
        n2_term(0, 1)
        for t in range(1, PACK):
            if t + 1 < PACK:
                n2_term(0, t + 1)
            add_n1_term(z_left[:, t, :], t, 0)
        z_left_rounded = round_all(nc.scalar.copy, z_left[:], "z_left_rounded")
        for t in range(1, PACK):
            n2_term(1, t)
        quantise(z_left_rounded, z_words, z_scales, 0)
        z_right = tile([P, 2, PACK, QUARTER], F32, "z_right", tag="z_left")
        for u in range(2):
            for t in range(PACK):
                add_n1_term(z_right[:, u, t, :], t, HALF + u * QUARTER)
        for u, copy in enumerate((nc.scalar.copy, nc.vector.tensor_copy)):
            quantise(round_all(copy, z_right[:, u], f"z_right_rounded{u}"), z_words, z_scales, HALF + u * QUARTER)

        sixteenth = [tile([P, 1], F32, f"sixteenth{u}") for u in range(2)]
        for factor in sixteenth:
            nc.gpsimd.memset(factor[:], 0.0625)
        minus_half = tile([P, 1], F32, "minus_half")
        nc.gpsimd.memset(minus_half[:], -0.5)
        ds = [tile([P, S], F32, f"ds{t}") for t in range(PACK)]

        def scores(t, lo, width, bank):
            cols = slice(lo, lo + width)
            acc = psum.tile([P, width], F32, name=f"acc_s{t}_{lo}", tag=f"bank{bank}")
            nc.tensor.matmul_mx(
                out=acc[:],
                lhsT=cand_dealt[:, P * t : P * (t + 1)].bitcast(FP8X4),
                lhsT_scale=cand_scales_dealt[:, P * t : P * (t + 1)],
                rhs=z_words[:, cols].bitcast(FP8X4),
                rhs_scale=z_scales[:, cols],
                start=True,
                stop=True,
            )
            nc.scalar.activation(ds[t][:, cols], acc[:], COPY, scale=sixteenth[t // 2][:])

        for t in range(PACK):
            scores(t, 0, HALF, PACK + t)
        scores(0, HALF, QUARTER, 0)
        scores(0, HALF + QUARTER, QUARTER, PACK)
        for t in range(1, PACK):
            scores(t, HALF, HALF, t)

        pa_first = tile([P, W], F32, "pa_first")
        early = tile([P, 3, W], F32, "early", tag="sixteenth0")
        late = tile([P, 2, 2, W], F32, "late", tag="sixteenth1")
        pairs = [
            (pa_first[:], early[:, 0, :]),
            (early[:, 1, :], early[:, 2, :]),
            (late[:, 0, 0, :], late[:, 0, 1, :]),
            (late[:, 1, 0, :], late[:, 1, 1, :]),
        ]
        neg_half_ds = {}

        def fetch_pair(t):
            pa, pb = pairs[t]
            nc.vector.tensor_copy(pa, ds[t][:].indirect(n3_sb[:]))
            nc.vector.tensor_scalar(pb, ds[t][:].indirect(n4_sb[:]), -0.5, 0.0, MULT, ADD)

        def put_back(t):
            pa, pb = pairs[t]
            nc.vector.tensor_tensor(ds[t][:].indirect(n4_sb[:]), pa, pb, ADD)
            scaled = tile([P, S], F32, f"neg_half_ds{t}")
            nc.scalar.activation(scaled[:], ds[t][:], COPY, scale=minus_half[:])
            neg_half_ds[t] = scaled

        fetch_pair(0)
        for t in range(1, PACK):
            fetch_pair(t)
            put_back(t - 1)
        put_back(PACK - 1)

        out_words = tile([P, S], U32, "out_words")
        out_scales = tile([P, S], U8, "out_scales")
        out_rows = out_0.rearrange("(p t) j -> p t j", t=PACK)
        words_dram = out_1[0].rearrange("p c r -> p (c r)").bitcast(I32)

        def fold(dst, t, lo):
            width = dst.shape[1]
            nc.vector.tensor_tensor(
                dst, neg_half_ds[t][:].indirect(entries(n5_sb, lo, width)), ds[t][:, lo : lo + width], ADD
            )

        def store_rows(values, first, last, lo):
            nc.sync.dma_start(out=out_rows[:, first : last + 1, lo : lo + HALF], in_=values[:, first : last + 1, :])

        out_left = tile([P, PACK, HALF], F32, "out_left")
        for t in range(PACK):
            fold(out_left[:, t, :], t, 0)
            if t % 2 == 1:
                store_rows(out_left, t - 1, t, 0)
        out_left_rounded = round_all(nc.scalar.copy, out_left[:], "out_left_rounded")
        out_right = tile([P, PACK, HALF], F32, "out_right", tag="minus_half")
        for t in range(PACK - 1):
            fold(out_right[:, t, :], t, HALF)
        store_rows(out_right, 0, PACK - 2, HALF)
        fold(out_right[:, PACK - 1, :], PACK - 1, HALF)
        store_rows(out_right, PACK - 1, PACK - 1, HALF)
        quantise(out_left_rounded[:, 0:QUARTER, :], out_words, out_scales, 0)
        out_right_rounded = tile([P, HALF, PACK], BF16, "out_right_rounded")
        for copy, lo, hi in ((nc.vector.tensor_copy, 0, VECTOR_COLS), (nc.scalar.copy, VECTOR_COLS, HALF)):
            round_columns(copy, out_right_rounded[:, lo:hi, :], out_right[:, :, lo:hi])
        quantise(out_left_rounded[:, QUARTER:HALF, :], out_words, out_scales, QUARTER)
        nc.sync.dma_start(out=words_dram[:, 0:HALF], in_=out_words[:, 0:HALF].bitcast(I32))
        quantise(out_right_rounded[:], out_words, out_scales, HALF)
        nc.sync.dma_start(out=words_dram[:, HALF:S], in_=out_words[:, HALF:S].bitcast(I32))
        for q in range(QUADRANTS):
            queue = nc.scalar if q % 2 else nc.sync
            queue.dma_start(
                out=out_2[0, PACK * q : PACK * (q + 1), :].bitcast(I32),
                in_=out_scales[QUADRANT * q : QUADRANT * q + PACK, :].bitcast(I32),
            )
